import numpy as np
import ml_dtypes


def mxq(x, axis, fmt="e4m3"):
    dtype, down = {"e4m3": (ml_dtypes.float8_e4m3fn, 7), "e5m2": (ml_dtypes.float8_e5m2, 14)}[fmt]
    v = np.moveaxis(np.asarray(x, np.float32).astype(ml_dtypes.bfloat16).astype(np.float64), axis, -1)
    blocks = v.reshape(v.shape[:-1] + (-1, 32))
    amax = np.abs(blocks).max(-1, keepdims=True)
    byte = np.maximum(np.where(amax > 0, np.frexp(amax)[1] - 1 + 127, 0) - down, 1)
    scale = np.exp2(byte - 127.0)
    codes = (blocks / scale).astype(np.float32).astype(dtype).astype(np.float64)
    return np.moveaxis((codes * scale).reshape(v.shape), -1, axis)


WIDE = False


def mx_kscale(k):
    if not WIDE:
        return np.ones(k)
    levels = np.array([10, -10, 5, -5, 0])
    if k % 512:
        return np.exp2(np.random.permutation(np.resize(levels, k // 32))).repeat(32)
    a = np.empty((k // 512, 16))
    for p in range(k // 512):
        a[p, :8] = np.random.permutation(np.resize(levels, 8))
        for g in range(8):
            far = levels[np.abs(levels - a[p, g]) >= 10]
            a[p, g + 8] = far[np.random.randint(len(far))]
    return np.exp2(a.ravel()).repeat(32)


def f64(x):
    return np.asarray(x).astype(np.float64)


def striped(idx):
    return np.tile(idx.reshape(-1, 16).T, (8, 1)).astype(np.uint16)


def unstriped(offs):
    return offs[:16].T.reshape(-1).astype(np.int64)


E2M1 = np.array([0.0, 0.5, 1.0, 1.5, 2.0, 3.0, 4.0, 6.0, -0.0, -0.5, -1.0, -1.5, -2.0, -3.0, -4.0, -6.0])


def pack_weight(w, fmt):
    k, n = w.shape
    w = f64(np.asarray(w, np.float32).astype(ml_dtypes.bfloat16)).reshape(k // 32, 32, n)
    amax = np.abs(w).max(1)
    if fmt == "e4m3":
        byte = np.frexp(amax)[1] - 1 + 127 - 7
    else:
        mant, ex = np.frexp(amax / 6.0)
        byte = np.where(mant > 0.5, ex, ex - 1) + 127
    byte = np.clip(np.where(amax > 0, byte, 1), 1, 254)
    scaled = (w * np.exp2(127.0 - byte)[:, None, :]).reshape(k, n).astype(np.float32)
    by_word = np.ascontiguousarray(scaled.reshape(k // 512, 128, 4, n).transpose(0, 1, 3, 2))
    if fmt == "e4m3":
        words = by_word.astype(ml_dtypes.float8_e4m3fn).view(np.uint8)
    else:
        c = by_word.astype(ml_dtypes.float4_e2m1fn).view(np.uint8) & 0xF
        words = (c[..., 0::2] | (c[..., 1::2] << 4)).reshape(k // 512, 128, 2 * n)
    return np.ascontiguousarray(words), np.ascontiguousarray(byte.astype(np.uint8).reshape(k // 512, 16, n))


def unpack_weight(words, scales, fmt):
    g, _, n = scales.shape
    words = np.ascontiguousarray(words).reshape(g, 128, n, -1)
    if fmt == "e4m3":
        vals = words.view(ml_dtypes.float8_e4m3fn).astype(np.float64)
    else:
        nib = np.empty((g, 128, n, 4), np.uint8)
        nib[..., 0::2] = words & 0xF
        nib[..., 1::2] = words >> 4
        vals = E2M1[nib]
    vals = vals * np.repeat(np.exp2(scales.astype(np.float64) - 127.0), 8, axis=1)[..., None]
    return vals.transpose(0, 1, 3, 2).reshape(g * 512, n)


K, T, E, C, N = 1536, 640, 20, 128, 128
TOP = 4


def by_expert(wq, xq):
    return np.concatenate([wq[e].T @ xq[:, e * C:(e + 1) * C] for e in range(E)], axis=1)


def setup_inputs():
    n = np.random.standard_normal
    s = mx_kscale(K)[:, None]
    deal = np.repeat(np.arange(E), C).reshape(TOP, T)[:, np.random.permutation(T)]
    deal = np.take_along_axis(deal, np.argsort(np.random.rand(TOP, T), axis=0), axis=0)
    for _ in range(8):
        s_, t_ = np.random.permutation(T).reshape(2, -1); r = np.random.randint(TOP, size=T // 2); x, y = deal[r, s_].copy(), deal[r, t_].copy()
        ok = ~((deal[:, s_] == y).any(0) | (deal[:, t_] == x).any(0)); deal[r[ok], s_[ok]] = y[ok]; deal[r[ok], t_[ok]] = x[ok]
    order = np.lexsort((np.random.rand(TOP * T), deal.reshape(-1)))
    slot_token = order % T; pos = np.empty(TOP * T, np.int64); pos[order] = np.arange(TOP * T); pos = pos.reshape(TOP, T)
    g = np.random.uniform(0.5, 1.5, (TOP, T)); g = g / g.sum(0)
    w = [pack_weight(m, "e2m1") for m in n((E + 1, K, N)) / np.sqrt(K) / s[None]]
    return {
        "xT": (n((K, T)) * s).astype(np.float32),
        "w_words": np.stack([m[0] for m in w]),
        "w_scales": np.stack([m[1] for m in w]),
        "gate": np.stack([np.tile(r, (N, 1)) for r in g]).astype(np.float32),
        "offs": striped(slot_token),
        "pos1": striped(pos[0]),
        "pos2": striped(pos[1]),
        "pos3": striped(pos[2]),
        "pos4": striped(pos[3]),
    }


def reference(xT, w_words, w_scales, gate, offs, pos1, pos2, pos3, pos4):
    idx = unstriped(offs)
    w = np.stack([unpack_weight(w_words[e], w_scales[e], "e2m1") for e in range(E + 1)])
    wq = w
    xs = mxq(f64(xT), 0, "e4m3")
    ys = wq[E].T @ xs
    xq = mxq(f64(xT)[:, idx], 0, "e4m3")
    y = by_expert(w, xq)
    return ys + sum(f64(gate[r]) * y[:, unstriped(p)] for r, p in enumerate((pos1, pos2, pos3, pos4)))

@@ -1,0 +1,220 @@
+from contextlib import ExitStack
+
+import concourse.mybir as mybir
+
+K, T, E, C, N = 1536, 640, 20, 128, 128
+TOP = 4
+S = E * C
+FLOPS = 2 * K * N * (S + T)
+
+F32 = mybir.dt.float32
+BF16 = mybir.dt.bfloat16
+I32 = mybir.dt.int32
+U32 = mybir.dt.uint32
+U16 = mybir.dt.uint16
+U8 = mybir.dt.uint8
+FP8X4 = mybir.dt.float8_e4m3fn_x4
+FP4X4 = mybir.dt.float4_e2m1fn_x4
+MULT = mybir.AluOpType.mult
+ADD = mybir.AluOpType.add
+COPY = mybir.ActivationFunctionType.Copy
+
+P = 128
+PASSES = K // 512
+WINDOW = 704
+CHUNK = 512
+LAST_PASS_CHUNKS = [512,512,512,512,256,128,128]
+SCALAR_SLOTS = 2048
+FIRST_CAST_VECTOR = 400
+TOKEN_PIECES = [(0, 512), (512, 128)]
+
+
+def tile_moe_shr_lin_none_kernel(tc, xT, w_words, w_scales, gate, offs, pos1, pos2, pos3, pos4, out):
+    nc = tc.nc
+    with ExitStack() as ctx:
+        keep = ctx.enter_context(tc.tile_pool(name="keep", bufs=1))
+        ring = ctx.enter_context(tc.tile_pool(name="ring", bufs=4))
+        psum = ctx.enter_context(tc.psum_pool(name="psum", bufs=4))
+        psum_shared = ctx.enter_context(tc.psum_pool(name="psum_shared", bufs=1))
+
+        halves = [(a, u) for a in range(PASSES) for u in range(2)]
+        raw = {h: keep.tile([P, 2, T], F32, name="raw%d%d" % h) for h in halves}
+        pairs = [keep.tile([P, 2, 2 * WINDOW], BF16, name="pairs%d" % a, align_bytes=64) for a in range(PASSES)]
+        slot_list = keep.tile([P, S // 16], U16, name="slot_list")
+        pos_lists = [keep.tile([P, T // 16], U16, name="pos_list%d" % r) for r in range(TOP)]
+        weights = keep.tile([P, (E + 1) * PASSES, 2 * N], U8, name="weights", align_bytes=64)
+        weight_scales = keep.tile([P, (E + 1) * PASSES, N], U8, name="weight_scales", align_bytes=64)
+        gates = keep.tile([P, TOP, T], F32, name="gates")
+        codes = [keep.tile([P, S], U32, name="codes%d" % a, align_bytes=64) for a in range(PASSES)]
+        scales = [keep.tile([P, S], U8, name="scales%d" % a, align_bytes=64) for a in range(PASSES)]
+        shared_grouped = [keep.tile([P, 4 * T], BF16, name="shared_grouped%d" % a, align_bytes=64) for a in range(PASSES)]
+        shared_codes = [keep.tile([P, T], U32, name="shared_codes%d" % a, align_bytes=64) for a in range(PASSES)]
+        shared_scales = [keep.tile([P, T], U8, name="shared_scales%d" % a, align_bytes=64) for a in range(PASSES)]
+        rows = keep.tile([P, 2, T], BF16, name="rows", align_bytes=64)
+        y = keep.tile([P, S], F32, name="y")
+
+        for a in range(PASSES):
+            nc.gpsimd.memset(pairs[a][:, :, 2 * T :], 0.0)
+        nc.gpsimd.memset(weight_scales[:].rearrange("p g n -> p (g n)").bitcast(I32), 0)
+
+        x_rows = xT.rearrange("(a p j) t -> a p j t", p=P, j=4)
+        for i, (a, u) in enumerate(halves):
+            nc.sync.dma_start(out=raw[a, u][:], in_=x_rows[a, :, 2 * u : 2 * u + 2, :])
+            if i == 0:
+                nc.sync.dma_start(slot_list[:], offs)
+        scale_rows = w_scales.rearrange("e a (q r) n -> r q (e a) n", r=4)
+        for r in range(4):
+            nc.sync.dma_start(out=weight_scales[r:P:32, :, :].bitcast(I32), in_=scale_rows[r].bitcast(I32))
+        weight_rows = w_words.rearrange("e a p b -> p (e a) b")
+        for g0 in range(0, (E + 1) * PASSES, 21):
+            nc.sync.dma_start(out=weights[:, g0 : g0 + 21, :].bitcast(I32), in_=weight_rows[:, g0 : g0 + 21, :].bitcast(I32))
+        for r, pos in enumerate((pos1, pos2, pos3, pos4)):
+            nc.sync.dma_start(pos_lists[r][:], pos)
+        nc.sync.dma_start(out=gates[:], in_=gate.rearrange("r p t -> p r t"))
+
+        def cast_views(h, t0, t1):
+            dst = pairs[h[0]][:, h[1], 2 * t0 : 2 * t1].rearrange("p (t e) -> p t e", e=2)
+            return dst, raw[h][:, :, t0:t1].rearrange("p e t -> p t e")
+
+        def cast(h):
+            dst, src = cast_views(h, 0, T)
+            nc.scalar.copy(dst, src)
+
+        staged = {}
+
+        def stage(a, s0, n):
+            if (a, s0) not in staged:
+                if a == PASSES - 1 and s0 < SCALAR_SLOTS:
+                    staged[a, s0] = keep.tile([P, 2, 2 * CHUNK], BF16, name="staged_late%d" % s0, align_bytes=64)
+                else:
+                    staged[a, s0] = ring.tile([P, 2, 2 * CHUNK], BF16, name="staged", align_bytes=64)
+            return staged[a, s0]
+
+        def gather(a, u, s0, n):
+            window = pairs[a][:, u, :].bitcast(U32)
+            dst = stage(a, s0, n)[:, u, 0 : 2 * n].bitcast(U32)
+            nc.vector.tensor_copy(dst, window.indirect(slot_list[:, s0 // 16 : (s0 + n) // 16]))
+
+        def gather_on_scalar(expert, e):
+            s0, c0 = expert * C // CHUNK * CHUNK, expert * C % CHUNK
+            tile = stage(PASSES - 1, s0, CHUNK)
+            offsets = slot_list[:, expert * C // 16 : (expert + 1) * C // 16]
+            nc.scalar.activation(tile[:, 1, 2 * c0 + e : 2 * (c0 + C) : 2], rows[:, e, :].indirect(offsets), COPY)
+
+        grouped = {}
+
+        def interleave(a, s0, n):
+            grouped[a, s0] = ring.tile([P, 4 * CHUNK], BF16, name="grouped", align_bytes=64)
+            dst = grouped[a, s0][:, 0 : 4 * n].bitcast(U32).rearrange("p (s u) -> p s u", u=2)
+            src = staged[a, s0][:, :, 0 : 2 * n].bitcast(U32).rearrange("p u s -> p s u")
+            nc.scalar.copy(dst, src)
+
+        def quantize(a, s0, n):
+            nc.vector.quantize_mx(
+                out=codes[a][:, s0 : s0 + n].bitcast(FP8X4),
+                scales=scales[a][:, s0 : s0 + n],
+                in_=grouped[a, s0][:, 0 : 4 * n],
+            )
+
+        def product(acc, e, all_codes, all_scales, s0, n):
+            for a in range(PASSES):
+                nc.tensor.matmul_mx(
+                    out=acc,
+                    lhsT=weights[:, e * PASSES + a, :].bitcast(FP4X4),
+                    lhsT_scale=weight_scales[:, e * PASSES + a, :],
+                    rhs=all_codes[a][:, s0 : s0 + n].bitcast(FP8X4),
+                    rhs_scale=all_scales[a][:, s0 : s0 + n],
+                    start=(a == 0),
+                    stop=(a == PASSES - 1),
+                )
+
+        def experts(s0, n):
+            acc = psum.tile([P, CHUNK], F32, name="acc")
+            for c0 in range(0, n, C):
+                product(acc[:, c0 : c0 + C], (s0 + c0) // C, codes, scales, s0 + c0, C)
+            nc.scalar.copy(y[:, s0 : s0 + n], acc[:, 0:n])
+
+        def shared_interleave(a):
+            dst = shared_grouped[a][:].bitcast(U32).rearrange("p (t u) -> p t u", u=2)
+            nc.scalar.copy(dst, pairs[a][:, :, 0 : 2 * T].bitcast(U32).rearrange("p u t -> p t u"))
+
+        def shared_quantize(a):
+            for t0, n in TOKEN_PIECES:
+                nc.vector.quantize_mx(
+                    out=shared_codes[a][:, t0 : t0 + n].bitcast(FP8X4),
+                    scales=shared_scales[a][:, t0 : t0 + n],
+                    in_=shared_grouped[a][:, 4 * t0 : 4 * (t0 + n)],
+                )
+
+        dst, src = cast_views((0, 0), 0, FIRST_CAST_VECTOR)
+        nc.vector.tensor_copy(dst, src)
+        dst, src = cast_views((0, 0), FIRST_CAST_VECTOR, T)
+        nc.scalar.activation(dst, src, COPY)
+        for h in halves[1:4]:
+            cast(h)
+
+        items = [(a, s0, CHUNK) for a in range(PASSES - 1) for s0 in range(0, S, CHUNK)]
+        s0 = 0
+        for n in LAST_PASS_CHUNKS:
+            items.append((PASSES - 1, s0, n))
+            s0 += n
+        scalar_experts = list(range(SCALAR_SLOTS // C))
+        lag = 2
+        head = 3
+        for a, s0, n in items[:head]:
+            gather(a, 0, s0, n)
+        for i in range(len(items) + lag):
+            if i < len(items):
+                a, s0, n = items[i]
+                if i >= head:
+                    gather(a, 0, s0, n)
+                if a == PASSES - 1 and s0 < SCALAR_SLOTS:
+                    if s0 + n > SCALAR_SLOTS:
+                        window = pairs[a][:, 1, :].bitcast(U32)
+                        part = stage(a, s0, n)[:, 1, 2 * (SCALAR_SLOTS - s0) : 2 * n].bitcast(U32)
+                        nc.vector.tensor_copy(part, window.indirect(slot_list[:, SCALAR_SLOTS // 16 : (s0 + n) // 16]))
+                else:
+                    gather(a, 1, s0, n)
+                interleave(a, s0, n)
+            if i == 1:
+                for h in halves[4:]:
+                    cast(h)
+                if scalar_experts:
+                    nc.scalar.copy(rows[:], raw[PASSES - 1, 1][:])
+            if 2 <= i < 10:
+                for e in range(2):
+                    for expert in scalar_experts[(i - 2) * len(scalar_experts) // 8 : (i - 1) * len(scalar_experts) // 8]:
+                        gather_on_scalar(expert, e)
+            if i in (11, 13, 14):
+                shared_interleave((11, 13, 14).index(i))
+            if i >= lag:
+                a, s0, n = items[i - lag]
+                quantize(a, s0, n)
+                if a == PASSES - 1:
+                    experts(s0, n)
+        for a in range(PASSES):
+            shared_quantize(a)
+        ys = {}
+        for t0, n in TOKEN_PIECES:
+            ys[t0] = psum_shared.tile([P, n], F32, name="ys%d" % t0)
+            product(ys[t0][:], E, shared_codes, shared_scales, t0, n)
+
+        picked = keep.tile([P, TOP, T], F32, name="picked")
+        total = keep.tile([P, TOP, T], F32, name="total")
+
+        def pick(r, t0, n):
+            offsets = pos_lists[r][:, t0 // 16 : (t0 + n) // 16]
+            nc.vector.tensor_tensor(picked[:, r, t0 : t0 + n], y[:].indirect(offsets), gates[:, r, t0 : t0 + n], MULT)
+
+        def add(r, t0, n):
+            before = ys[t0][:] if r == 0 else total[:, r - 1, t0 : t0 + n]
+            nc.vector.tensor_tensor(total[:, r, t0 : t0 + n], before, picked[:, r, t0 : t0 + n], ADD)
+            if r == TOP - 1:
+                nc.sync.dma_start(out=out[:, t0 : t0 + n], in_=total[:, r, t0 : t0 + n])
+
+        steps = [(r, t0, n) for t0, n in TOKEN_PIECES for r in range(TOP)]
+        for i in range(len(steps) + 1):
+            if i < len(steps):
+                pick(*steps[i])
+            if i >= 1:
+                add(*steps[i - 1])

@@ -23,9 +23,12 @@ P = 128
 PASSES = K // 512
 WINDOW = 704
 CHUNK = 512
-LAST_PASS_CHUNKS = [512,512,512,512,256,128,128]
-SCALAR_SLOTS = 2048
+LAST_PIECES = [256,128,128]
+LATE_CASTS = {0: [(2, 0)], 1: [(2, 1)]}
+SCALAR_EXPERTS = [0, 4, 4, 2, 2]
+HELPED = 1
 FIRST_CAST_VECTOR = 400
+SHARED_TAGS = ["shared0", "shared1", "last_codes"]
 TOKEN_PIECES = [(0, 512), (512, 128)]
 
 
@@ -34,10 +37,11 @@ def tile_moe_shr_lin_none_kernel(tc, xT, w_words, w_scales, gate, offs, pos1, po
     with ExitStack() as ctx:
         keep = ctx.enter_context(tc.tile_pool(name="keep", bufs=1))
         ring = ctx.enter_context(tc.tile_pool(name="ring", bufs=4))
+        stage_ring = ctx.enter_context(tc.tile_pool(name="stage_ring", bufs=4))
         psum = ctx.enter_context(tc.psum_pool(name="psum", bufs=4))
         psum_shared = ctx.enter_context(tc.psum_pool(name="psum_shared", bufs=1))
 
-        halves = [(a, u) for a in range(PASSES) for u in range(2)]
+        halves = [(0, 0), (0, 1), (1, 0), (1, 1), (2, 0), (2, 1)]
         raw = {h: keep.tile([P, 2, T], F32, name="raw%d%d" % h) for h in halves}
         pairs = [keep.tile([P, 2, 2 * WINDOW], BF16, name="pairs%d" % a, align_bytes=64) for a in range(PASSES)]
         slot_list = keep.tile([P, S // 16], U16, name="slot_list")
@@ -47,8 +51,7 @@ def tile_moe_shr_lin_none_kernel(tc, xT, w_words, w_scales, gate, offs, pos1, po
         gates = keep.tile([P, TOP, T], F32, name="gates")
         codes = [keep.tile([P, S], U32, name="codes%d" % a, align_bytes=64) for a in range(PASSES)]
         scales = [keep.tile([P, S], U8, name="scales%d" % a, align_bytes=64) for a in range(PASSES)]
-        shared_grouped = [keep.tile([P, 4 * T], BF16, name="shared_grouped%d" % a, align_bytes=64) for a in range(PASSES)]
-        shared_codes = [keep.tile([P, T], U32, name="shared_codes%d" % a, align_bytes=64) for a in range(PASSES)]
+        shared_grouped = {}
         shared_scales = [keep.tile([P, T], U8, name="shared_scales%d" % a, align_bytes=64) for a in range(PASSES)]
         rows = keep.tile([P, 2, T], BF16, name="rows", align_bytes=64)
         y = keep.tile([P, S], F32, name="y")
@@ -82,29 +85,30 @@ def tile_moe_shr_lin_none_kernel(tc, xT, w_words, w_scales, gate, offs, pos1, po
 
         staged = {}
 
-        def stage(a, s0, n):
+        def stage(a, s0):
             if (a, s0) not in staged:
-                if a == PASSES - 1 and s0 < SCALAR_SLOTS:
-                    staged[a, s0] = keep.tile([P, 2, 2 * CHUNK], BF16, name="staged_late%d" % s0, align_bytes=64)
-                else:
-                    staged[a, s0] = ring.tile([P, 2, 2 * CHUNK], BF16, name="staged", align_bytes=64)
+                staged[a, s0] = stage_ring.tile([P, 2, 2 * CHUNK], BF16, name="staged", align_bytes=64)
             return staged[a, s0]
 
-        def gather(a, u, s0, n):
+        def gather(a, u, s0, n, skip=0):
             window = pairs[a][:, u, :].bitcast(U32)
-            dst = stage(a, s0, n)[:, u, 0 : 2 * n].bitcast(U32)
-            nc.vector.tensor_copy(dst, window.indirect(slot_list[:, s0 // 16 : (s0 + n) // 16]))
+            dst = stage(a, s0)[:, u, 2 * skip : 2 * n].bitcast(U32)
+            nc.vector.tensor_copy(dst, window.indirect(slot_list[:, (s0 + skip) // 16 : (s0 + n) // 16]))
 
-        def gather_on_scalar(expert, e):
-            s0, c0 = expert * C // CHUNK * CHUNK, expert * C % CHUNK
-            tile = stage(PASSES - 1, s0, CHUNK)
-            offsets = slot_list[:, expert * C // 16 : (expert + 1) * C // 16]
-            nc.scalar.activation(tile[:, 1, 2 * c0 + e : 2 * (c0 + C) : 2], rows[:, e, :].indirect(offsets), COPY)
+        def gather_on_scalar(s0):
+            tile = stage(HELPED, s0)
+            for e in range(2):
+                for c0 in range(0, C * SCALAR_EXPERTS[s0 // CHUNK], C):
+                    offsets = slot_list[:, (s0 + c0) // 16 : (s0 + c0 + C) // 16]
+                    nc.scalar.activation(tile[:, 1, 2 * c0 + e : 2 * (c0 + C) : 2], rows[:, e, :].indirect(offsets), COPY)
 
         grouped = {}
 
         def interleave(a, s0, n):
-            grouped[a, s0] = ring.tile([P, 4 * CHUNK], BF16, name="grouped", align_bytes=64)
+            if (a, s0) == (PASSES - 1, S - C):
+                grouped[a, s0] = keep.tile([P, 4 * C], BF16, name="last_grouped", tag="late", align_bytes=64)
+            else:
+                grouped[a, s0] = ring.tile([P, 4 * CHUNK], BF16, name="grouped", align_bytes=64)
             dst = grouped[a, s0][:, 0 : 4 * n].bitcast(U32).rearrange("p (s u) -> p s u", u=2)
             src = staged[a, s0][:, :, 0 : 2 * n].bitcast(U32).rearrange("p u s -> p s u")
             nc.scalar.copy(dst, src)
@@ -116,8 +120,8 @@ def tile_moe_shr_lin_none_kernel(tc, xT, w_words, w_scales, gate, offs, pos1, po
                 in_=grouped[a, s0][:, 0 : 4 * n],
             )
 
-        def product(acc, e, all_codes, all_scales, s0, n):
-            for a in range(PASSES):
+        def product(acc, e, all_codes, all_scales, s0, n, passes=range(PASSES)):
+            for a in passes:
                 nc.tensor.matmul_mx(
                     out=acc,
                     lhsT=weights[:, e * PASSES + a, :].bitcast(FP4X4),
@@ -128,13 +132,24 @@ def tile_moe_shr_lin_none_kernel(tc, xT, w_words, w_scales, gate, offs, pos1, po
                     stop=(a == PASSES - 1),
                 )
 
+        begun = {}
+
+        def begin(s0):
+            begun[s0] = psum_shared.tile([P, C], F32, name="begun%d" % s0)
+            product(begun[s0][:], s0 // C, codes, scales, s0, C, range(PASSES - 1))
+
         def experts(s0, n):
-            acc = psum.tile([P, CHUNK], F32, name="acc")
-            for c0 in range(0, n, C):
-                product(acc[:, c0 : c0 + C], (s0 + c0) // C, codes, scales, s0 + c0, C)
+            if s0 in begun:
+                acc = begun[s0]
+                product(acc[:], s0 // C, codes, scales, s0, C, [PASSES - 1])
+            else:
+                acc = psum.tile([P, CHUNK], F32, name="acc")
+                for c0 in range(0, n, C):
+                    product(acc[:, c0 : c0 + C], (s0 + c0) // C, codes, scales, s0 + c0, C)
             nc.scalar.copy(y[:, s0 : s0 + n], acc[:, 0:n])
 
         def shared_interleave(a):
+            shared_grouped[a] = keep.tile([P, 4 * T], BF16, name="shared_grouped", tag="shared%d" % a, align_bytes=64)
             dst = shared_grouped[a][:].bitcast(U32).rearrange("p (t u) -> p t u", u=2)
             nc.scalar.copy(dst, pairs[a][:, :, 0 : 2 * T].bitcast(U32).rearrange("p u t -> p t u"))
 
@@ -150,15 +165,12 @@ def tile_moe_shr_lin_none_kernel(tc, xT, w_words, w_scales, gate, offs, pos1, po
         nc.vector.tensor_copy(dst, src)
         dst, src = cast_views((0, 0), FIRST_CAST_VECTOR, T)
         nc.scalar.activation(dst, src, COPY)
-        for h in halves[1:4]:
-            cast(h)
+        cast((0, 1))
+        cast((1, 0))
+        cast((1, 1))
 
-        items = [(a, s0, CHUNK) for a in range(PASSES - 1) for s0 in range(0, S, CHUNK)]
-        s0 = 0
-        for n in LAST_PASS_CHUNKS:
-            items.append((PASSES - 1, s0, n))
-            s0 += n
-        scalar_experts = list(range(SCALAR_SLOTS // C))
+        items = [(0, s0, CHUNK) for s0 in range(0, S, CHUNK)]
+        items += [(1, 0, 512), (2, 0, 512), (1, 512, 512), (2, 512, 512), (1, 1024, 512), (2, 1024, 512), (1, 1536, 512), (1, 2048, 512), (2, 1536, 256), (2, 1792, 256), (2, 2048, 256), (2, 2304, 128), (2, 2432, 128)]
         lag = 2
         head = 3
         for a, s0, n in items[:head]:
@@ -168,53 +180,65 @@ def tile_moe_shr_lin_none_kernel(tc, xT, w_words, w_scales, gate, offs, pos1, po
                 a, s0, n = items[i]
                 if i >= head:
                     gather(a, 0, s0, n)
-                if a == PASSES - 1 and s0 < SCALAR_SLOTS:
-                    if s0 + n > SCALAR_SLOTS:
-                        window = pairs[a][:, 1, :].bitcast(U32)
-                        part = stage(a, s0, n)[:, 1, 2 * (SCALAR_SLOTS - s0) : 2 * n].bitcast(U32)
-                        nc.vector.tensor_copy(part, window.indirect(slot_list[:, SCALAR_SLOTS // 16 : (s0 + n) // 16]))
-                else:
-                    gather(a, 1, s0, n)
+                skip = C * SCALAR_EXPERTS[s0 // CHUNK] if a == HELPED else 0
+                if skip < n:
+                    gather(a, 1, s0, n, skip)
                 interleave(a, s0, n)
-            if i == 1:
-                for h in halves[4:]:
-                    cast(h)
-                if scalar_experts:
-                    nc.scalar.copy(rows[:], raw[PASSES - 1, 1][:])
-            if 2 <= i < 10:
-                for e in range(2):
-                    for expert in scalar_experts[(i - 2) * len(scalar_experts) // 8 : (i - 1) * len(scalar_experts) // 8]:
-                        gather_on_scalar(expert, e)
-            if i in (11, 13, 14):
-                shared_interleave((11, 13, 14).index(i))
+            for h in LATE_CASTS.get(i, []):
+                cast(h)
+            if i == 3:
+                nc.scalar.copy(rows[:], raw[HELPED, 1][:])
+            if i + 2 < len(items) and items[i + 2][0] == HELPED:
+                gather_on_scalar(items[i + 2][1])
             if i >= lag:
                 a, s0, n = items[i - lag]
                 quantize(a, s0, n)
                 if a == PASSES - 1:
                     experts(s0, n)
+                if (a, s0) == (1, S - CHUNK):
+                    begin(S - 2 * C)
+                    begin(S - C)
+            if i in (9, 11, 13):
+                shared_interleave((9, 11, 13).index(i))
+        shared_words = keep.tile([P, PASSES, T], U32, name="shared_words", tag="late", align_bytes=64)
+        shared_codes = [shared_words[:, a, :] for a in range(PASSES)]
         for a in range(PASSES):
             shared_quantize(a)
-        ys = {}
-        for t0, n in TOKEN_PIECES:
-            ys[t0] = psum_shared.tile([P, n], F32, name="ys%d" % t0)
-            product(ys[t0][:], E, shared_codes, shared_scales, t0, n)
 
         picked = keep.tile([P, TOP, T], F32, name="picked")
         total = keep.tile([P, TOP, T], F32, name="total")
+        ys = {}
+
+        def shared_products():
+            for t0, n in TOKEN_PIECES:
+                ys[t0] = psum_shared.tile([P, n], F32, name="ys%d" % t0)
+                product(ys[t0][:], E, shared_codes, shared_scales, t0, n)
 
         def pick(r, t0, n):
             offsets = pos_lists[r][:, t0 // 16 : (t0 + n) // 16]
             nc.vector.tensor_tensor(picked[:, r, t0 : t0 + n], y[:].indirect(offsets), gates[:, r, t0 : t0 + n], MULT)
 
-        def add(r, t0, n):
-            before = ys[t0][:] if r == 0 else total[:, r - 1, t0 : t0 + n]
-            nc.vector.tensor_tensor(total[:, r, t0 : t0 + n], before, picked[:, r, t0 : t0 + n], ADD)
-            if r == TOP - 1:
-                nc.sync.dma_start(out=out[:, t0 : t0 + n], in_=total[:, r, t0 : t0 + n])
+        def add(step, first, second, t0, n):
+            nc.vector.tensor_tensor(total[:, step, t0 : t0 + n], first, second, ADD)
+            if step == TOP - 1:
+                nc.sync.dma_start(out=out[:, t0 : t0 + n], in_=total[:, step, t0 : t0 + n])
 
-        steps = [(r, t0, n) for t0, n in TOKEN_PIECES for r in range(TOP)]
-        for i in range(len(steps) + 1):
-            if i < len(steps):
-                pick(*steps[i])
-            if i >= 1:
-                add(*steps[i - 1])
+        (t0, n), (t1, m) = TOKEN_PIECES
+        first, second = slice(t0, t0 + n), slice(t1, t1 + m)
+        shared_products()
+        pick(0, t0, n)
+        pick(1, t0, n)
+        add(0, picked[:, 0, first], picked[:, 1, first], t0, n)
+        pick(2, t0, n)
+        pick(3, t0, n)
+        add(1, total[:, 0, first], picked[:, 2, first], t0, n)
+        pick(0, t1, m)
+        add(2, total[:, 1, first], picked[:, 3, first], t0, n)
+        pick(1, t1, m)
+        add(3, ys[t0][:], total[:, 2, first], t0, n)
+        add(0, ys[t1][:], picked[:, 0, second], t1, m)
+        pick(2, t1, m)
+        add(1, total[:, 0, second], picked[:, 1, second], t1, m)
+        pick(3, t1, m)
+        add(2, total[:, 1, second], picked[:, 2, second], t1, m)
+        add(3, total[:, 2, second], picked[:, 3, second], t1, m)

@@ -24,9 +24,10 @@ PASSES = K // 512
 WINDOW = 704
 CHUNK = 512
 LAST_PIECES = [256,128,128]
-LATE_CASTS = {0: [(2, 0)], 1: [(2, 1)]}
-SCALAR_EXPERTS = [0, 4, 4, 2, 2]
+LATE_CASTS = {}
+SCALAR_EXPERTS = [4, 4, 4, 4, 2]
 HELPED = 1
+SCALAR_GATHERS_AT = [0, 2, 5, 7, 9]
 FIRST_CAST_VECTOR = 400
 SHARED_TAGS = ["shared0", "shared1", "last_codes"]
 TOKEN_PIECES = [(0, 512), (512, 128)]
@@ -36,20 +37,21 @@ def tile_moe_shr_lin_none_kernel(tc, xT, w_words, w_scales, gate, offs, pos1, po
     nc = tc.nc
     with ExitStack() as ctx:
         keep = ctx.enter_context(tc.tile_pool(name="keep", bufs=1))
-        ring = ctx.enter_context(tc.tile_pool(name="ring", bufs=4))
-        stage_ring = ctx.enter_context(tc.tile_pool(name="stage_ring", bufs=4))
+        ring = ctx.enter_context(tc.tile_pool(name="ring", bufs=6))
+        stage_ring = ctx.enter_context(tc.tile_pool(name="stage_ring", bufs=3))
+        helped_ring = ctx.enter_context(tc.tile_pool(name="helped_ring", bufs=2))
         psum = ctx.enter_context(tc.psum_pool(name="psum", bufs=4))
         psum_shared = ctx.enter_context(tc.psum_pool(name="psum_shared", bufs=1))
 
-        halves = [(0, 0), (0, 1), (1, 0), (1, 1), (2, 0), (2, 1)]
-        raw = {h: keep.tile([P, 2, T], F32, name="raw%d%d" % h) for h in halves}
+        halves = [(0, 0), (0, 1), (1, 1), (1, 0), (2, 0), (2, 1)]
+        raw = {h: keep.tile([P, 2, T], F32, name="raw", tag="raw%d%d" % h, align_bytes=64) for h in halves}
         pairs = [keep.tile([P, 2, 2 * WINDOW], BF16, name="pairs%d" % a, align_bytes=64) for a in range(PASSES)]
         slot_list = keep.tile([P, S // 16], U16, name="slot_list")
         pos_lists = [keep.tile([P, T // 16], U16, name="pos_list%d" % r) for r in range(TOP)]
         weights = keep.tile([P, (E + 1) * PASSES, 2 * N], U8, name="weights", align_bytes=64)
         weight_scales = keep.tile([P, (E + 1) * PASSES, N], U8, name="weight_scales", align_bytes=64)
         gates = keep.tile([P, TOP, T], F32, name="gates")
-        codes = [keep.tile([P, S], U32, name="codes%d" % a, align_bytes=64) for a in range(PASSES)]
+        codes = {a: keep.tile([P, S], U32, name="codes%d" % a, align_bytes=64) for a in range(1, PASSES)}
         scales = [keep.tile([P, S], U8, name="scales%d" % a, align_bytes=64) for a in range(PASSES)]
         shared_grouped = {}
         shared_scales = [keep.tile([P, T], U8, name="shared_scales%d" % a, align_bytes=64) for a in range(PASSES)]
@@ -57,8 +59,8 @@ def tile_moe_shr_lin_none_kernel(tc, xT, w_words, w_scales, gate, offs, pos1, po
         y = keep.tile([P, S], F32, name="y")
 
         for a in range(PASSES):
-            nc.gpsimd.memset(pairs[a][:, :, 2 * T :], 0.0)
-        nc.gpsimd.memset(weight_scales[:].rearrange("p g n -> p (g n)").bitcast(I32), 0)
+            nc.vector.memset(pairs[a][:, :, 2 * T :], 0.0)
+        nc.vector.memset(weight_scales[:].rearrange("p g n -> p (g n)").bitcast(I32), 0)
 
         x_rows = xT.rearrange("(a p j) t -> a p j t", p=P, j=4)
         for i, (a, u) in enumerate(halves):
@@ -83,11 +85,16 @@ def tile_moe_shr_lin_none_kernel(tc, xT, w_words, w_scales, gate, offs, pos1, po
             dst, src = cast_views(h, 0, T)
             nc.scalar.copy(dst, src)
 
+        def cast_on_gpsimd(h):
+            dst, src = cast_views(h, 0, T)
+            nc.gpsimd.tensor_scalar(dst, src, 1.0, 0.0, MULT, ADD)
+
         staged = {}
 
         def stage(a, s0):
             if (a, s0) not in staged:
-                staged[a, s0] = stage_ring.tile([P, 2, 2 * CHUNK], BF16, name="staged", align_bytes=64)
+                pool = helped_ring if a == HELPED else stage_ring
+                staged[a, s0] = pool.tile([P, 2, 2 * CHUNK], BF16, name="staged", align_bytes=64)
             return staged[a, s0]
 
         def gather(a, u, s0, n, skip=0):
@@ -166,9 +173,11 @@ def tile_moe_shr_lin_none_kernel(tc, xT, w_words, w_scales, gate, offs, pos1, po
         dst, src = cast_views((0, 0), FIRST_CAST_VECTOR, T)
         nc.scalar.activation(dst, src, COPY)
         cast((0, 1))
-        cast((1, 0))
-        cast((1, 1))
+        nc.scalar.copy(rows[:], raw[HELPED, 1][:])
+        for h in halves[2:]:
+            cast_on_gpsimd(h)
 
+        codes[0] = keep.tile([P, S], U32, name="codes0", tag="raw%d%d" % halves[-1], align_bytes=64)
         items = [(0, s0, CHUNK) for s0 in range(0, S, CHUNK)]
         items += [(1, 0, 512), (2, 0, 512), (1, 512, 512), (2, 512, 512), (1, 1024, 512), (2, 1024, 512), (1, 1536, 512), (1, 2048, 512), (2, 1536, 256), (2, 1792, 256), (2, 2048, 256), (2, 2304, 128), (2, 2432, 128)]
         lag = 2
@@ -186,10 +195,10 @@ def tile_moe_shr_lin_none_kernel(tc, xT, w_words, w_scales, gate, offs, pos1, po
                 interleave(a, s0, n)
             for h in LATE_CASTS.get(i, []):
                 cast(h)
-            if i == 3:
+            if i == -1:
                 nc.scalar.copy(rows[:], raw[HELPED, 1][:])
-            if i + 2 < len(items) and items[i + 2][0] == HELPED:
-                gather_on_scalar(items[i + 2][1])
+            if i in SCALAR_GATHERS_AT:
+                gather_on_scalar(CHUNK * SCALAR_GATHERS_AT.index(i))
             if i >= lag:
                 a, s0, n = items[i - lag]
                 quantize(a, s0, n)

@@ -21,15 +21,29 @@ COPY = mybir.ActivationFunctionType.Copy
 
 P = 128
 PASSES = K // 512
-WINDOW = 704
+LAST = PASSES - 1
 CHUNK = 512
-LAST_PIECES = [256,128,128]
-LATE_CASTS = {}
-SCALAR_EXPERTS = [4, 4, 4, 4, 2]
-HELPED = 1
-SCALAR_GATHERS_AT = [0, 2, 5, 7, 9]
+WINDOW = 704
+WEIGHT_ROWS = 21
+
+LOAD_ORDER = [(0, 0), (0, 1), (1, 1), (2, 0), (1, 0), (2, 1)]
 FIRST_CAST_VECTOR = 400
-SHARED_TAGS = ["shared0", "shared1", "last_codes"]
+
+PIECES = (
+    [(0, s0, CHUNK) for s0 in range(0, S, CHUNK)]
+    + [(a, s0, CHUNK) for s0 in range(0, S - CHUNK, CHUNK) for a in (1, 2)]
+    + [(1, S - CHUNK, CHUNK), (2, S - CHUNK, 2 * C), (2, S - 2 * C, C), (2, S - C, C)]
+)
+HELPED = 1
+SCALAR_EXPERTS = [[1, 2, 1, 2, 1], [4, 4, 4, 0, 3]]
+SCALAR_GATHER_STEPS = [1, 3, 6, 7, 13]
+FIRST_GATHERS = 2
+LAST_STEPS = 3
+
+GROUPED_BUFS = 8
+STAGED_BUFS = [4, 3, 3]
+ACC_BUFS = 4
+
 TOKEN_PIECES = [(0, 512), (512, 128)]
 
 
@@ -37,130 +51,174 @@ def tile_moe_shr_lin_none_kernel(tc, xT, w_words, w_scales, gate, offs, pos1, po
     nc = tc.nc
     with ExitStack() as ctx:
         keep = ctx.enter_context(tc.tile_pool(name="keep", bufs=1))
-        ring = ctx.enter_context(tc.tile_pool(name="ring", bufs=6))
-        stage_ring = ctx.enter_context(tc.tile_pool(name="stage_ring", bufs=3))
-        helped_ring = ctx.enter_context(tc.tile_pool(name="helped_ring", bufs=2))
-        psum = ctx.enter_context(tc.psum_pool(name="psum", bufs=4))
-        psum_shared = ctx.enter_context(tc.psum_pool(name="psum_shared", bufs=1))
+        grouped_ring = ctx.enter_context(tc.tile_pool(name="ring", bufs=GROUPED_BUFS))
+        staged_ring2 = ctx.enter_context(tc.tile_pool(name="stage_ring", bufs=STAGED_BUFS[2]))
+        staged_ring1 = ctx.enter_context(tc.tile_pool(name="helped_ring", bufs=STAGED_BUFS[1]))
+        staged_ring0 = ctx.enter_context(tc.tile_pool(name="first_ring", bufs=STAGED_BUFS[0]))
+        staged_rings = [staged_ring0, staged_ring1, staged_ring2]
+        psum = ctx.enter_context(tc.psum_pool(name="psum", bufs=ACC_BUFS))
+        psum_keep = ctx.enter_context(tc.psum_pool(name="psum_shared", bufs=1))
 
-        halves = [(0, 0), (0, 1), (1, 1), (1, 0), (2, 0), (2, 1)]
-        raw = {h: keep.tile([P, 2, T], F32, name="raw", tag="raw%d%d" % h, align_bytes=64) for h in halves}
-        pairs = [keep.tile([P, 2, 2 * WINDOW], BF16, name="pairs%d" % a, align_bytes=64) for a in range(PASSES)]
+        raw_pass = [keep.tile([P, 4, T], F32, name="raw", tag="raw%d" % a, align_bytes=64) for a in range(PASSES)]
+        raw = {(a, u): raw_pass[a][:, 2 * u : 2 * u + 2, :] for a, u in LOAD_ORDER}
+        pairs_pass = [keep.tile([P, 2, 2 * WINDOW], BF16, name="pairs%d" % a, align_bytes=64) for a in range(PASSES)]
+        pairs = {(a, u): pairs_pass[a][:, u, :] for a, u in LOAD_ORDER}
         slot_list = keep.tile([P, S // 16], U16, name="slot_list")
         pos_lists = [keep.tile([P, T // 16], U16, name="pos_list%d" % r) for r in range(TOP)]
         weights = keep.tile([P, (E + 1) * PASSES, 2 * N], U8, name="weights", align_bytes=64)
         weight_scales = keep.tile([P, (E + 1) * PASSES, N], U8, name="weight_scales", align_bytes=64)
         gates = keep.tile([P, TOP, T], F32, name="gates")
-        codes = {a: keep.tile([P, S], U32, name="codes%d" % a, align_bytes=64) for a in range(1, PASSES)}
-        scales = [keep.tile([P, S], U8, name="scales%d" % a, align_bytes=64) for a in range(PASSES)]
-        shared_grouped = {}
+        slot_codes = [keep.tile([P, S], U32, name="codes%d" % a, align_bytes=64) for a in range(PASSES)]
         shared_scales = [keep.tile([P, T], U8, name="shared_scales%d" % a, align_bytes=64) for a in range(PASSES)]
-        rows = keep.tile([P, 2, T], BF16, name="rows", align_bytes=64)
+        rows = keep.tile([P, 4, T], BF16, name="rows", align_bytes=64)
         y = keep.tile([P, S], F32, name="y")
 
         for a in range(PASSES):
-            nc.vector.memset(pairs[a][:, :, 2 * T :], 0.0)
+            nc.vector.memset(pairs_pass[a][:, :, 2 * T :], 0.0)
         nc.vector.memset(weight_scales[:].rearrange("p g n -> p (g n)").bitcast(I32), 0)
 
         x_rows = xT.rearrange("(a p j) t -> a p j t", p=P, j=4)
-        for i, (a, u) in enumerate(halves):
-            nc.sync.dma_start(out=raw[a, u][:], in_=x_rows[a, :, 2 * u : 2 * u + 2, :])
-            if i == 0:
+        for a, u in LOAD_ORDER:
+            nc.sync.dma_start(out=raw[a, u], in_=x_rows[a, :, 2 * u : 2 * u + 2, :])
+            if (a, u) == LOAD_ORDER[0]:
                 nc.sync.dma_start(slot_list[:], offs)
         scale_rows = w_scales.rearrange("e a (q r) n -> r q (e a) n", r=4)
         for r in range(4):
             nc.sync.dma_start(out=weight_scales[r:P:32, :, :].bitcast(I32), in_=scale_rows[r].bitcast(I32))
         weight_rows = w_words.rearrange("e a p b -> p (e a) b")
-        for g0 in range(0, (E + 1) * PASSES, 21):
-            nc.sync.dma_start(out=weights[:, g0 : g0 + 21, :].bitcast(I32), in_=weight_rows[:, g0 : g0 + 21, :].bitcast(I32))
+        for g0 in range(0, (E + 1) * PASSES, WEIGHT_ROWS):
+            group = slice(g0, g0 + WEIGHT_ROWS)
+            nc.sync.dma_start(out=weights[:, group, :].bitcast(I32), in_=weight_rows[:, group, :].bitcast(I32))
         for r, pos in enumerate((pos1, pos2, pos3, pos4)):
             nc.sync.dma_start(pos_lists[r][:], pos)
         nc.sync.dma_start(out=gates[:], in_=gate.rearrange("r p t -> p r t"))
 
-        def cast_views(h, t0, t1):
-            dst = pairs[h[0]][:, h[1], 2 * t0 : 2 * t1].rearrange("p (t e) -> p t e", e=2)
-            return dst, raw[h][:, :, t0:t1].rearrange("p e t -> p t e")
 
-        def cast(h):
-            dst, src = cast_views(h, 0, T)
-            nc.scalar.copy(dst, src)
+        def pair_views(half, t0, t1):
+            dst = pairs[half][:, 2 * t0 : 2 * t1].rearrange("p (t e) -> p t e", e=2)
+            return dst, raw[half][:, :, t0:t1].rearrange("p e t -> p t e")
 
-        def cast_on_gpsimd(h):
-            dst, src = cast_views(h, 0, T)
+        def round_on_gpsimd(dst, src):
             nc.gpsimd.tensor_scalar(dst, src, 1.0, 0.0, MULT, ADD)
+
+        shared_grouped = {}
+
+        def round_shared(a):
+            shared_grouped[a] = keep.tile([P, 4 * T], BF16, name="shared_grouped", tag="shared%d" % a, align_bytes=64)
+            round_on_gpsimd(shared_grouped[a][:].rearrange("p (t j) -> p t j", j=4), raw_pass[a][:].rearrange("p j t -> p t j"))
+
+        dst, src = pair_views((0, 0), 0, FIRST_CAST_VECTOR)
+        nc.vector.tensor_copy(dst, src)
+        dst, src = pair_views((0, 0), FIRST_CAST_VECTOR, T)
+        nc.scalar.activation(dst, src, COPY)
+        nc.scalar.copy(rows[:, 2:4, :], raw[HELPED, 1])
+        round_on_gpsimd(*pair_views((0, 1), 0, T))
+        round_on_gpsimd(*pair_views((1, 1), 0, T))
+        round_shared(0)
+        round_on_gpsimd(*pair_views((2, 0), 0, T))
+        round_on_gpsimd(*pair_views((2, 1), 0, T))
+        round_on_gpsimd(*pair_views((1, 0), 0, T))
+        round_on_gpsimd(rows[:, 0:2, :], raw[HELPED, 0])
+        round_shared(1)
+        round_shared(2)
+
+        slot_scale_planes = keep.tile([P, PASSES, S], U8, name="scales", tag="raw1", align_bytes=64)
+        slot_scales = [slot_scale_planes[:, a, :] for a in range(PASSES)]
+
 
         staged = {}
 
         def stage(a, s0):
             if (a, s0) not in staged:
-                pool = helped_ring if a == HELPED else stage_ring
-                staged[a, s0] = pool.tile([P, 2, 2 * CHUNK], BF16, name="staged", align_bytes=64)
+                staged[a, s0] = staged_rings[a].tile([P, 2, 2 * CHUNK], BF16, name="staged", align_bytes=64)
             return staged[a, s0]
 
-        def gather(a, u, s0, n, skip=0):
-            window = pairs[a][:, u, :].bitcast(U32)
+        def gather_on_vector(a, u, s0, n, skip):
             dst = stage(a, s0)[:, u, 2 * skip : 2 * n].bitcast(U32)
-            nc.vector.tensor_copy(dst, window.indirect(slot_list[:, (s0 + skip) // 16 : (s0 + n) // 16]))
+            offsets = slot_list[:, (s0 + skip) // 16 : (s0 + n) // 16]
+            nc.vector.tensor_copy(dst, pairs[a, u].bitcast(U32).indirect(offsets))
 
-        def gather_on_scalar(s0):
+        def gather_on_scalar(chunk):
+            s0 = chunk * CHUNK
             tile = stage(HELPED, s0)
-            for e in range(2):
-                for c0 in range(0, C * SCALAR_EXPERTS[s0 // CHUNK], C):
-                    offsets = slot_list[:, (s0 + c0) // 16 : (s0 + c0 + C) // 16]
-                    nc.scalar.activation(tile[:, 1, 2 * c0 + e : 2 * (c0 + C) : 2], rows[:, e, :].indirect(offsets), COPY)
+            for u in (1, 0):
+                for e in range(2):
+                    for c0 in range(0, C * SCALAR_EXPERTS[u][chunk], C):
+                        offsets = slot_list[:, (s0 + c0) // 16 : (s0 + c0 + C) // 16]
+                        dst = tile[:, u, 2 * c0 + e : 2 * (c0 + C) : 2]
+                        nc.scalar.activation(dst, rows[:, 2 * u + e, :].indirect(offsets), COPY)
 
         grouped = {}
 
         def interleave(a, s0, n):
-            if (a, s0) == (PASSES - 1, S - C):
+            if (a, s0, n) == PIECES[-1]:
                 grouped[a, s0] = keep.tile([P, 4 * C], BF16, name="last_grouped", tag="late", align_bytes=64)
+                dst = grouped[a, s0][:, 0 : 4 * n].rearrange("p (s u e) -> p s u e", u=2, e=2)
+                nc.vector.tensor_copy(dst, staged[a, s0][:, :, 0 : 2 * n].rearrange("p u (s e) -> p s u e", e=2))
             else:
-                grouped[a, s0] = ring.tile([P, 4 * CHUNK], BF16, name="grouped", align_bytes=64)
-            dst = grouped[a, s0][:, 0 : 4 * n].bitcast(U32).rearrange("p (s u) -> p s u", u=2)
-            src = staged[a, s0][:, :, 0 : 2 * n].bitcast(U32).rearrange("p u s -> p s u")
-            nc.scalar.copy(dst, src)
+                grouped[a, s0] = grouped_ring.tile([P, 4 * CHUNK], BF16, name="grouped", align_bytes=64)
+                dst = grouped[a, s0][:, 0 : 4 * n].bitcast(U32).rearrange("p (s u) -> p s u", u=2)
+                nc.scalar.copy(dst, staged[a, s0][:, :, 0 : 2 * n].bitcast(U32).rearrange("p u s -> p s u"))
 
-        def quantize(a, s0, n):
-            nc.vector.quantize_mx(
-                out=codes[a][:, s0 : s0 + n].bitcast(FP8X4),
-                scales=scales[a][:, s0 : s0 + n],
-                in_=grouped[a, s0][:, 0 : 4 * n],
-            )
-
-        def product(acc, e, all_codes, all_scales, s0, n, passes=range(PASSES)):
+        def product(acc, expert, codes, scales, first, n, passes):
             for a in passes:
                 nc.tensor.matmul_mx(
                     out=acc,
-                    lhsT=weights[:, e * PASSES + a, :].bitcast(FP4X4),
-                    lhsT_scale=weight_scales[:, e * PASSES + a, :],
-                    rhs=all_codes[a][:, s0 : s0 + n].bitcast(FP8X4),
-                    rhs_scale=all_scales[a][:, s0 : s0 + n],
+                    lhsT=weights[:, expert * PASSES + a, :].bitcast(FP4X4),
+                    lhsT_scale=weight_scales[:, expert * PASSES + a, :],
+                    rhs=codes[a][:, first : first + n].bitcast(FP8X4),
+                    rhs_scale=scales[a][:, first : first + n],
                     start=(a == 0),
-                    stop=(a == PASSES - 1),
+                    stop=(a == LAST),
                 )
 
         begun = {}
 
-        def begin(s0):
-            begun[s0] = psum_shared.tile([P, C], F32, name="begun%d" % s0)
-            product(begun[s0][:], s0 // C, codes, scales, s0, C, range(PASSES - 1))
+        def begin_expert(s0):
+            begun[s0] = psum_keep.tile([P, C], F32, name="begun%d" % s0)
+            product(begun[s0][:], s0 // C, slot_codes, slot_scales, s0, C, range(LAST))
 
-        def experts(s0, n):
+        def finish_experts(s0, n):
             if s0 in begun:
-                acc = begun[s0]
-                product(acc[:], s0 // C, codes, scales, s0, C, [PASSES - 1])
-            else:
-                acc = psum.tile([P, CHUNK], F32, name="acc")
-                for c0 in range(0, n, C):
-                    product(acc[:, c0 : c0 + C], (s0 + c0) // C, codes, scales, s0 + c0, C)
-            nc.scalar.copy(y[:, s0 : s0 + n], acc[:, 0:n])
+                product(begun[s0][:], s0 // C, slot_codes, slot_scales, s0, C, [LAST])
+                return begun[s0]
+            acc = psum.tile([P, CHUNK], F32, name="acc")
+            for c0 in range(0, n, C):
+                product(acc[:, c0 : c0 + C], (s0 + c0) // C, slot_codes, slot_scales, s0 + c0, C, range(PASSES))
+            return acc
 
-        def shared_interleave(a):
-            shared_grouped[a] = keep.tile([P, 4 * T], BF16, name="shared_grouped", tag="shared%d" % a, align_bytes=64)
-            dst = shared_grouped[a][:].bitcast(U32).rearrange("p (t u) -> p t u", u=2)
-            nc.scalar.copy(dst, pairs[a][:, :, 0 : 2 * T].bitcast(U32).rearrange("p u t -> p t u"))
+        for a, s0, n in PIECES[:FIRST_GATHERS]:
+            gather_on_vector(a, 0, s0, n, 0)
+        in_psum = []
+        for step in range(len(PIECES) + 1):
+            if step in SCALAR_GATHER_STEPS:
+                gather_on_scalar(SCALAR_GATHER_STEPS.index(step))
+            if step < len(PIECES):
+                a, s0, n = PIECES[step]
+                for u in range(1 if step < FIRST_GATHERS else 0, 2):
+                    skip = C * SCALAR_EXPERTS[u][s0 // CHUNK] if a == HELPED else 0
+                    if skip < n:
+                        gather_on_vector(a, u, s0, n, skip)
+                interleave(a, s0, n)
+            if step >= 1:
+                a, s0, n = PIECES[step - 1]
+                nc.vector.quantize_mx(
+                    out=slot_codes[a][:, s0 : s0 + n].bitcast(FP8X4),
+                    scales=slot_scales[a][:, s0 : s0 + n],
+                    in_=grouped[a, s0][:, 0 : 4 * n],
+                )
+                if a == LAST:
+                    in_psum.append((s0, n, finish_experts(s0, n)))
+                while len(in_psum) > (1 if step < len(PIECES) - LAST_STEPS else 0):
+                    y0, width, acc = in_psum.pop(0)
+                    nc.scalar.copy(y[:, y0 : y0 + width], acc[:, 0:width])
+                if (a, s0) == (LAST - 1, S - CHUNK):
+                    begin_expert(S - 2 * C)
+                    begin_expert(S - C)
 
-        def shared_quantize(a):
+        shared_code_planes = keep.tile([P, PASSES, T], U32, name="shared_words", tag="late", align_bytes=64)
+        shared_codes = [shared_code_planes[:, a, :] for a in range(PASSES)]
+        for a in range(PASSES):
             for t0, n in TOKEN_PIECES:
                 nc.vector.quantize_mx(
                     out=shared_codes[a][:, t0 : t0 + n].bitcast(FP8X4),
@@ -168,86 +226,37 @@ def tile_moe_shr_lin_none_kernel(tc, xT, w_words, w_scales, gate, offs, pos1, po
                     in_=shared_grouped[a][:, 4 * t0 : 4 * (t0 + n)],
                 )
 
-        dst, src = cast_views((0, 0), 0, FIRST_CAST_VECTOR)
-        nc.vector.tensor_copy(dst, src)
-        dst, src = cast_views((0, 0), FIRST_CAST_VECTOR, T)
-        nc.scalar.activation(dst, src, COPY)
-        cast((0, 1))
-        nc.scalar.copy(rows[:], raw[HELPED, 1][:])
-        for h in halves[2:]:
-            cast_on_gpsimd(h)
+        picked = keep.tile([P, TOP, T], F32, name="picked", tag="raw0", align_bytes=64)
+        total = keep.tile([P, TOP, T], F32, name="total", tag="raw1", align_bytes=64)
+        ys = []
+        for t0, n in TOKEN_PIECES:
+            ys.append(psum_keep.tile([P, n], F32, name="ys%d" % t0))
+            product(ys[-1][:], E, shared_codes, shared_scales, t0, n, range(PASSES))
 
-        codes[0] = keep.tile([P, S], U32, name="codes0", tag="raw%d%d" % halves[-1], align_bytes=64)
-        items = [(0, s0, CHUNK) for s0 in range(0, S, CHUNK)]
-        items += [(1, 0, 512), (2, 0, 512), (1, 512, 512), (2, 512, 512), (1, 1024, 512), (2, 1024, 512), (1, 1536, 512), (1, 2048, 512), (2, 1536, 256), (2, 1792, 256), (2, 2048, 256), (2, 2304, 128), (2, 2432, 128)]
-        lag = 2
-        head = 3
-        for a, s0, n in items[:head]:
-            gather(a, 0, s0, n)
-        for i in range(len(items) + lag):
-            if i < len(items):
-                a, s0, n = items[i]
-                if i >= head:
-                    gather(a, 0, s0, n)
-                skip = C * SCALAR_EXPERTS[s0 // CHUNK] if a == HELPED else 0
-                if skip < n:
-                    gather(a, 1, s0, n, skip)
-                interleave(a, s0, n)
-            for h in LATE_CASTS.get(i, []):
-                cast(h)
-            if i == -1:
-                nc.scalar.copy(rows[:], raw[HELPED, 1][:])
-            if i in SCALAR_GATHERS_AT:
-                gather_on_scalar(CHUNK * SCALAR_GATHERS_AT.index(i))
-            if i >= lag:
-                a, s0, n = items[i - lag]
-                quantize(a, s0, n)
-                if a == PASSES - 1:
-                    experts(s0, n)
-                if (a, s0) == (1, S - CHUNK):
-                    begin(S - 2 * C)
-                    begin(S - C)
-            if i in (9, 11, 13):
-                shared_interleave((9, 11, 13).index(i))
-        shared_words = keep.tile([P, PASSES, T], U32, name="shared_words", tag="late", align_bytes=64)
-        shared_codes = [shared_words[:, a, :] for a in range(PASSES)]
-        for a in range(PASSES):
-            shared_quantize(a)
 
-        picked = keep.tile([P, TOP, T], F32, name="picked")
-        total = keep.tile([P, TOP, T], F32, name="total")
-        ys = {}
+        def pick(r, tokens):
+            offsets = pos_lists[r][:, tokens.start // 16 : tokens.stop // 16]
+            nc.vector.tensor_tensor(picked[:, r, tokens], y[:].indirect(offsets), gates[:, r, tokens], MULT)
 
-        def shared_products():
-            for t0, n in TOKEN_PIECES:
-                ys[t0] = psum_shared.tile([P, n], F32, name="ys%d" % t0)
-                product(ys[t0][:], E, shared_codes, shared_scales, t0, n)
+        def add(i, tokens, left, right):
+            nc.vector.tensor_tensor(total[:, i, tokens], left, right, ADD)
+            if i == TOP - 1:
+                nc.sync.dma_start(out=out[:, tokens], in_=total[:, i, tokens])
 
-        def pick(r, t0, n):
-            offsets = pos_lists[r][:, t0 // 16 : (t0 + n) // 16]
-            nc.vector.tensor_tensor(picked[:, r, t0 : t0 + n], y[:].indirect(offsets), gates[:, r, t0 : t0 + n], MULT)
-
-        def add(step, first, second, t0, n):
-            nc.vector.tensor_tensor(total[:, step, t0 : t0 + n], first, second, ADD)
-            if step == TOP - 1:
-                nc.sync.dma_start(out=out[:, t0 : t0 + n], in_=total[:, step, t0 : t0 + n])
-
-        (t0, n), (t1, m) = TOKEN_PIECES
-        first, second = slice(t0, t0 + n), slice(t1, t1 + m)
-        shared_products()
-        pick(0, t0, n)
-        pick(1, t0, n)
-        add(0, picked[:, 0, first], picked[:, 1, first], t0, n)
-        pick(2, t0, n)
-        pick(3, t0, n)
-        add(1, total[:, 0, first], picked[:, 2, first], t0, n)
-        pick(0, t1, m)
-        add(2, total[:, 1, first], picked[:, 3, first], t0, n)
-        pick(1, t1, m)
-        add(3, ys[t0][:], total[:, 2, first], t0, n)
-        add(0, ys[t1][:], picked[:, 0, second], t1, m)
-        pick(2, t1, m)
-        add(1, total[:, 0, second], picked[:, 1, second], t1, m)
-        pick(3, t1, m)
-        add(2, total[:, 1, second], picked[:, 2, second], t1, m)
-        add(3, total[:, 2, second], picked[:, 3, second], t1, m)
+        wide, narrow = [slice(t0, t0 + n) for t0, n in TOKEN_PIECES]
+        pick(0, wide)
+        pick(1, wide)
+        add(0, wide, picked[:, 0, wide], picked[:, 1, wide])
+        pick(2, wide)
+        pick(3, wide)
+        add(1, wide, total[:, 0, wide], picked[:, 2, wide])
+        pick(0, narrow)
+        add(2, wide, total[:, 1, wide], picked[:, 3, wide])
+        pick(1, narrow)
+        add(3, wide, ys[0][:], total[:, 2, wide])
+        add(0, narrow, ys[1][:], picked[:, 0, narrow])
+        pick(2, narrow)
+        add(1, narrow, total[:, 0, narrow], picked[:, 1, narrow])
+        pick(3, narrow)
+        add(2, narrow, total[:, 1, narrow], picked[:, 2, narrow])
+        add(3, narrow, total[:, 2, narrow], picked[:, 3, narrow])

from contextlib import ExitStack

import concourse.mybir as mybir

K, T, E, C, N = 1536, 640, 20, 128, 128
TOP = 4
S = E * C
FLOPS = 2 * K * N * (S + T)

F32 = mybir.dt.float32
BF16 = mybir.dt.bfloat16
I32 = mybir.dt.int32
U32 = mybir.dt.uint32
U16 = mybir.dt.uint16
U8 = mybir.dt.uint8
FP8X4 = mybir.dt.float8_e4m3fn_x4
FP4X4 = mybir.dt.float4_e2m1fn_x4
MULT = mybir.AluOpType.mult
ADD = mybir.AluOpType.add
COPY = mybir.ActivationFunctionType.Copy

P = 128
PASSES = K // 512
LAST = PASSES - 1
CHUNK = 512
WINDOW = 704
WEIGHT_ROWS = 21

LOAD_ORDER = [(0, 0), (0, 1), (1, 1), (2, 0), (1, 0), (2, 1)]
FIRST_CAST_VECTOR = 400

PIECES = (
    [(0, s0, CHUNK) for s0 in range(0, S, CHUNK)]
    + [(a, s0, CHUNK) for s0 in range(0, S - CHUNK, CHUNK) for a in (1, 2)]
    + [(1, S - CHUNK, CHUNK), (2, S - CHUNK, 2 * C), (2, S - 2 * C, C), (2, S - C, C)]
)
HELPED = 1
SCALAR_EXPERTS = [[1, 2, 1, 2, 1], [4, 4, 4, 0, 3]]
SCALAR_GATHER_STEPS = [1, 3, 6, 7, 13]
FIRST_GATHERS = 2
LAST_STEPS = 3

GROUPED_BUFS = 8
STAGED_BUFS = [4, 3, 3]
ACC_BUFS = 4

TOKEN_PIECES = [(0, 512), (512, 128)]


def tile_moe_shr_lin_none_kernel(tc, xT, w_words, w_scales, gate, offs, pos1, pos2, pos3, pos4, out):
    nc = tc.nc
    with ExitStack() as ctx:
        keep = ctx.enter_context(tc.tile_pool(name="keep", bufs=1))
        grouped_ring = ctx.enter_context(tc.tile_pool(name="ring", bufs=GROUPED_BUFS))
        staged_ring2 = ctx.enter_context(tc.tile_pool(name="stage_ring", bufs=STAGED_BUFS[2]))
        staged_ring1 = ctx.enter_context(tc.tile_pool(name="helped_ring", bufs=STAGED_BUFS[1]))
        staged_ring0 = ctx.enter_context(tc.tile_pool(name="first_ring", bufs=STAGED_BUFS[0]))
        staged_rings = [staged_ring0, staged_ring1, staged_ring2]
        psum = ctx.enter_context(tc.psum_pool(name="psum", bufs=ACC_BUFS))
        psum_keep = ctx.enter_context(tc.psum_pool(name="psum_shared", bufs=1))

        raw_pass = [keep.tile([P, 4, T], F32, name="raw", tag="raw%d" % a, align_bytes=64) for a in range(PASSES)]
        raw = {(a, u): raw_pass[a][:, 2 * u : 2 * u + 2, :] for a, u in LOAD_ORDER}
        pairs_pass = [keep.tile([P, 2, 2 * WINDOW], BF16, name="pairs%d" % a, align_bytes=64) for a in range(PASSES)]
        pairs = {(a, u): pairs_pass[a][:, u, :] for a, u in LOAD_ORDER}
        slot_list = keep.tile([P, S // 16], U16, name="slot_list")
        pos_lists = [keep.tile([P, T // 16], U16, name="pos_list%d" % r) for r in range(TOP)]
        weights = keep.tile([P, (E + 1) * PASSES, 2 * N], U8, name="weights", align_bytes=64)
        weight_scales = keep.tile([P, (E + 1) * PASSES, N], U8, name="weight_scales", align_bytes=64)
        gates = keep.tile([P, TOP, T], F32, name="gates")
        slot_codes = [keep.tile([P, S], U32, name="codes%d" % a, align_bytes=64) for a in range(PASSES)]
        shared_scales = [keep.tile([P, T], U8, name="shared_scales%d" % a, align_bytes=64) for a in range(PASSES)]
        rows = keep.tile([P, 4, T], BF16, name="rows", align_bytes=64)
        y = keep.tile([P, S], F32, name="y")

        for a in range(PASSES):
            nc.vector.memset(pairs_pass[a][:, :, 2 * T :], 0.0)
        nc.vector.memset(weight_scales[:].rearrange("p g n -> p (g n)").bitcast(I32), 0)

        x_rows = xT.rearrange("(a p j) t -> a p j t", p=P, j=4)
        for a, u in LOAD_ORDER:
            nc.sync.dma_start(out=raw[a, u], in_=x_rows[a, :, 2 * u : 2 * u + 2, :])
            if (a, u) == LOAD_ORDER[0]:
                nc.sync.dma_start(slot_list[:], offs)
        scale_rows = w_scales.rearrange("e a (q r) n -> r q (e a) n", r=4)
        for r in range(4):
            nc.sync.dma_start(out=weight_scales[r:P:32, :, :].bitcast(I32), in_=scale_rows[r].bitcast(I32))
        weight_rows = w_words.rearrange("e a p b -> p (e a) b")
        for g0 in range(0, (E + 1) * PASSES, WEIGHT_ROWS):
            group = slice(g0, g0 + WEIGHT_ROWS)
            nc.sync.dma_start(out=weights[:, group, :].bitcast(I32), in_=weight_rows[:, group, :].bitcast(I32))
        for r, pos in enumerate((pos1, pos2, pos3, pos4)):
            nc.sync.dma_start(pos_lists[r][:], pos)
        nc.sync.dma_start(out=gates[:], in_=gate.rearrange("r p t -> p r t"))


        def pair_views(half, t0, t1):
            dst = pairs[half][:, 2 * t0 : 2 * t1].rearrange("p (t e) -> p t e", e=2)
            return dst, raw[half][:, :, t0:t1].rearrange("p e t -> p t e")

        def round_on_gpsimd(dst, src):
            nc.gpsimd.tensor_scalar(dst, src, 1.0, 0.0, MULT, ADD)

        shared_grouped = {}

        def round_shared(a):
            shared_grouped[a] = keep.tile([P, 4 * T], BF16, name="shared_grouped", tag="shared%d" % a, align_bytes=64)
            round_on_gpsimd(shared_grouped[a][:].rearrange("p (t j) -> p t j", j=4), raw_pass[a][:].rearrange("p j t -> p t j"))

        dst, src = pair_views((0, 0), 0, FIRST_CAST_VECTOR)
        nc.vector.tensor_copy(dst, src)
        dst, src = pair_views((0, 0), FIRST_CAST_VECTOR, T)
        nc.scalar.activation(dst, src, COPY)
        nc.scalar.copy(rows[:, 2:4, :], raw[HELPED, 1])
        round_on_gpsimd(*pair_views((0, 1), 0, T))
        round_on_gpsimd(*pair_views((1, 1), 0, T))
        round_shared(0)
        round_on_gpsimd(*pair_views((2, 0), 0, T))
        round_on_gpsimd(*pair_views((2, 1), 0, T))
        round_on_gpsimd(*pair_views((1, 0), 0, T))
        round_on_gpsimd(rows[:, 0:2, :], raw[HELPED, 0])
        round_shared(1)
        round_shared(2)

        slot_scale_planes = keep.tile([P, PASSES, S], U8, name="scales", tag="raw1", align_bytes=64)
        slot_scales = [slot_scale_planes[:, a, :] for a in range(PASSES)]


        staged = {}

        def stage(a, s0):
            if (a, s0) not in staged:
                staged[a, s0] = staged_rings[a].tile([P, 2, 2 * CHUNK], BF16, name="staged", align_bytes=64)
            return staged[a, s0]

        def gather_on_vector(a, u, s0, n, skip):
            dst = stage(a, s0)[:, u, 2 * skip : 2 * n].bitcast(U32)
            offsets = slot_list[:, (s0 + skip) // 16 : (s0 + n) // 16]
            nc.vector.tensor_copy(dst, pairs[a, u].bitcast(U32).indirect(offsets))

        def gather_on_scalar(chunk):
            s0 = chunk * CHUNK
            tile = stage(HELPED, s0)
            for u in (1, 0):
                for e in range(2):
                    for c0 in range(0, C * SCALAR_EXPERTS[u][chunk], C):
                        offsets = slot_list[:, (s0 + c0) // 16 : (s0 + c0 + C) // 16]
                        dst = tile[:, u, 2 * c0 + e : 2 * (c0 + C) : 2]
                        nc.scalar.activation(dst, rows[:, 2 * u + e, :].indirect(offsets), COPY)

        grouped = {}

        def interleave(a, s0, n):
            if (a, s0, n) == PIECES[-1]:
                grouped[a, s0] = keep.tile([P, 4 * C], BF16, name="last_grouped", tag="late", align_bytes=64)
                dst = grouped[a, s0][:, 0 : 4 * n].rearrange("p (s u e) -> p s u e", u=2, e=2)
                nc.vector.tensor_copy(dst, staged[a, s0][:, :, 0 : 2 * n].rearrange("p u (s e) -> p s u e", e=2))
            else:
                grouped[a, s0] = grouped_ring.tile([P, 4 * CHUNK], BF16, name="grouped", align_bytes=64)
                dst = grouped[a, s0][:, 0 : 4 * n].bitcast(U32).rearrange("p (s u) -> p s u", u=2)
                nc.scalar.copy(dst, staged[a, s0][:, :, 0 : 2 * n].bitcast(U32).rearrange("p u s -> p s u"))

        def product(acc, expert, codes, scales, first, n, passes):
            for a in passes:
                nc.tensor.matmul_mx(
                    out=acc,
                    lhsT=weights[:, expert * PASSES + a, :].bitcast(FP4X4),
                    lhsT_scale=weight_scales[:, expert * PASSES + a, :],
                    rhs=codes[a][:, first : first + n].bitcast(FP8X4),
                    rhs_scale=scales[a][:, first : first + n],
                    start=(a == 0),
                    stop=(a == LAST),
                )

        begun = {}

        def begin_expert(s0):
            begun[s0] = psum_keep.tile([P, C], F32, name="begun%d" % s0)
            product(begun[s0][:], s0 // C, slot_codes, slot_scales, s0, C, range(LAST))

        def finish_experts(s0, n):
            if s0 in begun:
                product(begun[s0][:], s0 // C, slot_codes, slot_scales, s0, C, [LAST])
                return begun[s0]
            acc = psum.tile([P, CHUNK], F32, name="acc")
            for c0 in range(0, n, C):
                product(acc[:, c0 : c0 + C], (s0 + c0) // C, slot_codes, slot_scales, s0 + c0, C, range(PASSES))
            return acc

        for a, s0, n in PIECES[:FIRST_GATHERS]:
            gather_on_vector(a, 0, s0, n, 0)
        in_psum = []
        for step in range(len(PIECES) + 1):
            if step in SCALAR_GATHER_STEPS:
                gather_on_scalar(SCALAR_GATHER_STEPS.index(step))
            if step < len(PIECES):
                a, s0, n = PIECES[step]
                for u in range(1 if step < FIRST_GATHERS else 0, 2):
                    skip = C * SCALAR_EXPERTS[u][s0 // CHUNK] if a == HELPED else 0
                    if skip < n:
                        gather_on_vector(a, u, s0, n, skip)
                interleave(a, s0, n)
            if step >= 1:
                a, s0, n = PIECES[step - 1]
                nc.vector.quantize_mx(
                    out=slot_codes[a][:, s0 : s0 + n].bitcast(FP8X4),
                    scales=slot_scales[a][:, s0 : s0 + n],
                    in_=grouped[a, s0][:, 0 : 4 * n],
                )
                if a == LAST:
                    in_psum.append((s0, n, finish_experts(s0, n)))
                while len(in_psum) > (1 if step < len(PIECES) - LAST_STEPS else 0):
                    y0, width, acc = in_psum.pop(0)
                    nc.scalar.copy(y[:, y0 : y0 + width], acc[:, 0:width])
                if (a, s0) == (LAST - 1, S - CHUNK):
                    begin_expert(S - 2 * C)
                    begin_expert(S - C)

        shared_code_planes = keep.tile([P, PASSES, T], U32, name="shared_words", tag="late", align_bytes=64)
        shared_codes = [shared_code_planes[:, a, :] for a in range(PASSES)]
        for a in range(PASSES):
            for t0, n in TOKEN_PIECES:
                nc.vector.quantize_mx(
                    out=shared_codes[a][:, t0 : t0 + n].bitcast(FP8X4),
                    scales=shared_scales[a][:, t0 : t0 + n],
                    in_=shared_grouped[a][:, 4 * t0 : 4 * (t0 + n)],
                )

        picked = keep.tile([P, TOP, T], F32, name="picked", tag="raw0", align_bytes=64)
        total = keep.tile([P, TOP, T], F32, name="total", tag="raw1", align_bytes=64)
        ys = []
        for t0, n in TOKEN_PIECES:
            ys.append(psum_keep.tile([P, n], F32, name="ys%d" % t0))
            product(ys[-1][:], E, shared_codes, shared_scales, t0, n, range(PASSES))


        def pick(r, tokens):
            offsets = pos_lists[r][:, tokens.start // 16 : tokens.stop // 16]
            nc.vector.tensor_tensor(picked[:, r, tokens], y[:].indirect(offsets), gates[:, r, tokens], MULT)

        def add(i, tokens, left, right):
            nc.vector.tensor_tensor(total[:, i, tokens], left, right, ADD)
            if i == TOP - 1:
                nc.sync.dma_start(out=out[:, tokens], in_=total[:, i, tokens])

        wide, narrow = [slice(t0, t0 + n) for t0, n in TOKEN_PIECES]
        pick(0, wide)
        pick(1, wide)
        add(0, wide, picked[:, 0, wide], picked[:, 1, wide])
        pick(2, wide)
        pick(3, wide)
        add(1, wide, total[:, 0, wide], picked[:, 2, wide])
        pick(0, narrow)
        add(2, wide, total[:, 1, wide], picked[:, 3, wide])
        pick(1, narrow)
        add(3, wide, ys[0][:], total[:, 2, wide])
        add(0, narrow, ys[1][:], picked[:, 0, narrow])
        pick(2, narrow)
        add(1, narrow, total[:, 0, narrow], picked[:, 1, narrow])
        pick(3, narrow)
        add(2, narrow, total[:, 1, narrow], picked[:, 2, narrow])
        add(3, narrow, total[:, 2, narrow], picked[:, 3, narrow])
